import numpy as np
import ml_dtypes


def mxq(x, axis, fmt="e4m3"):
    dtype, down = {"e4m3": (ml_dtypes.float8_e4m3fn, 7), "e5m2": (ml_dtypes.float8_e5m2, 14)}[fmt]
    v = np.moveaxis(np.asarray(x, np.float32).astype(ml_dtypes.bfloat16).astype(np.float64), axis, -1)
    blocks = v.reshape(v.shape[:-1] + (-1, 32))
    amax = np.abs(blocks).max(-1, keepdims=True)
    byte = np.maximum(np.where(amax > 0, np.frexp(amax)[1] - 1 + 127, 0) - down, 1)
    scale = np.exp2(byte - 127.0)
    codes = (blocks / scale).astype(np.float32).astype(dtype).astype(np.float64)
    return np.moveaxis((codes * scale).reshape(v.shape), -1, axis)


WIDE = False


def mx_kscale(k):
    if not WIDE:
        return np.ones(k)
    levels = np.array([10, -10, 5, -5, 0])
    if k % 512:
        return np.exp2(np.random.permutation(np.resize(levels, k // 32))).repeat(32)
    a = np.empty((k // 512, 16))
    for p in range(k // 512):
        a[p, :8] = np.random.permutation(np.resize(levels, 8))
        for g in range(8):
            far = levels[np.abs(levels - a[p, g]) >= 10]
            a[p, g + 8] = far[np.random.randint(len(far))]
    return np.exp2(a.ravel()).repeat(32)


def f64(x):
    return np.asarray(x).astype(np.float64)


def striped(idx):
    return np.tile(np.asarray(idx).reshape(-1, 16).T, (8, 1)).astype(np.uint16)


def unstriped(offs):
    return offs[:16].T.reshape(-1).astype(np.int64)


B, N, C, D, NQ = 1, 1024, 4096, 512, 128
SEG = 64


def eight(codes):
    return np.concatenate([codes[h].reshape(-1, 16).T for h in range(8)]).astype(np.uint16)


def uneight(offs):
    return np.stack([offs[16 * h:16 * h + 16].T.reshape(-1) for h in range(8)]).astype(np.int64)


def setup_inputs():
    n = np.random.standard_normal
    s = mx_kscale(D)[:, None]
    grid = lambda x: np.round(x * 32) / 32
    return {
        "qT": (n((B, D, NQ)) * s / np.sqrt(D)).astype(np.float32),
        "cb": (grid(n((D, C))) / s).astype(np.float32),
        "norm": np.tile(np.random.randint(32, 129, N) / 64.0, (128, 1)).astype(np.float32),
        "offs": eight(np.random.randint(0, C, (8, N))),
    }


def reference(qT, cb, norm, offs):
    k = []
    for part, offs_ in enumerate((offs,)):
        codes = uneight(offs_)
        k += [f64(cb)[512 * part + 64 * h:512 * part + 64 * h + 64][:, codes[h]] for h in range(8)]
    k = np.concatenate(k) * f64(norm)[:1]
    a = mxq(f64(qT), 1, "e4m3").transpose(0, 2, 1) @ mxq(k, 0, "e4m3")
    return a.reshape(B, NQ, N // SEG, SEG).max(-1)

from contextlib import ExitStack

import concourse.mybir as mybir
from concourse.masks import make_identity

P = 128
PLANES = 4
D = P * PLANES
C = 4096
N = 1024
NQ = 128
SEG = 64
LIST_ROWS = 16
NORM_RUN = 8
BANK = 512

WIDTHS = (128, 256, 256, 256, 128)

FLOPS = 2 * D * N * NQ

F32 = mybir.dt.float32
BF16 = mybir.dt.bfloat16
U32 = mybir.dt.uint32
U16 = mybir.dt.uint16
U8 = mybir.dt.uint8
FP8X4 = mybir.dt.float8_e4m3fn_x4
MULT = mybir.AluOpType.mult
MAX = mybir.AluOpType.max
AXIS_X = mybir.AxisListType.X


def tile_attend_pq_max64_kernel(tc, qT, cb, norm, offs, out):
    nc = tc.nc
    with ExitStack() as ctx:
        keep = ctx.enter_context(tc.tile_pool(name="keep", bufs=1))
        psum = ctx.enter_context(tc.psum_pool(name="psum", bufs=1))

        offsets = keep.tile([P, N // LIST_ROWS], U16, name="offsets")
        nc.sync.dma_start(offsets[:], offs)

        norm_cols = keep.tile([P, NORM_RUN], F32, name="norm_cols")
        nc.sync.dma_start(norm_cols[:], norm[0:1, :].rearrange("o (p j) -> (o p) j", j=NORM_RUN))

        q_raw = keep.tile([P, PLANES, NQ], F32, name="q_raw")
        planes = [keep.tile([P, C], F32, name=f"plane{t}") for t in range(PLANES)]
        cb_planes = cb.rearrange("(p t) c -> p t c", t=PLANES)
        nc.sync.dma_start(planes[0][:], cb_planes[:, 0, :])
        nc.sync.dma_start(q_raw[:], qT[0].rearrange("(p t) q -> p t q", t=PLANES))
        for t in range(1, PLANES):
            nc.sync.dma_start(planes[t][:], cb_planes[:, t, :])

        ident = keep.tile([P, P], F32, name="ident")
        make_identity(nc, ident[:])
        norm_all = keep.tile([P, N], F32, name="norm_all")
        norm_view = norm_all[:].rearrange("i (p j) -> i p j", j=NORM_RUN)
        per_bank = BANK // P
        for b in range(NORM_RUN // per_bank):
            spread = psum.tile([P, per_bank, P], F32, name=f"spread{b}")
            for j in range(per_bank):
                col = b * per_bank + j
                nc.tensor.transpose(spread[:, j, :], norm_cols[:, col:col + 1].to_broadcast([P, P]), ident[:])
            nc.scalar.copy(norm_view[:, :, b * per_bank:(b + 1) * per_bank], spread[:].rearrange("i j p -> i p j"))

        q_words = keep.tile([P, NQ, PLANES], BF16, name="q_words", align_bytes=64)
        q_codes = keep.tile([P, NQ], U32, name="q_codes", align_bytes=64)
        q_scales = keep.tile([P, NQ], U8, name="q_scales", align_bytes=64)
        nc.vector.tensor_copy(q_words[:], q_raw[:].rearrange("p t q -> p q t"))
        nc.vector.quantize_mx(
            out=q_codes[:].bitcast(FP8X4), scales=q_scales[:], in_=q_words[:].rearrange("p q t -> p (q t)")
        )

        starts = [sum(WIDTHS[:i]) for i in range(len(WIDTHS))]
        picked01 = keep.tile([P, 2, N], F32, name="picked01")
        picked2 = keep.tile([P, N], F32, name="picked2")
        picked3 = keep.tile([P, N], F32, name="picked3")
        k_words = [keep.tile([P, w, PLANES], BF16, name=f"k_words{i}", align_bytes=64) for i, w in enumerate(WIDTHS)]

        def gather(dst, t, i):
            c0, c1 = starts[i], starts[i] + WIDTHS[i]
            nc.vector.tensor_tensor(
                dst, planes[t][:].indirect(offsets[:, c0 // LIST_ROWS:c1 // LIST_ROWS]), norm_all[:, c0:c1], MULT
            )

        pieces = range(len(WIDTHS))
        cols = [slice(starts[i], starts[i] + WIDTHS[i]) for i in pieces]
        for t in (0, 1):
            for i in pieces:
                gather(picked01[:, t, cols[i]], t, i)
        for i in pieces:
            nc.vector.tensor_copy(k_words[i][:, :, 0:2], picked01[:, :, cols[i]].rearrange("p t n -> p n t"))
        for t, picked in ((2, picked2), (3, picked3)):
            for i in pieces:
                gather(picked[:, cols[i]], t, i)
            for i in pieces:
                nc.scalar.copy(k_words[i][:, :, t], picked[:, cols[i]])

        best = keep.tile([P, N // SEG], F32, name="best")
        scores = []

        def multiply(i):
            w = WIDTHS[i]
            codes = keep.tile([P, w], U32, name=f"k_codes{i}", align_bytes=64)
            scales = keep.tile([P, w], U8, name=f"k_scales{i}", align_bytes=64)
            nc.vector.quantize_mx(
                out=codes[:].bitcast(FP8X4), scales=scales[:], in_=k_words[i][:].rearrange("p n t -> p (n t)")
            )
            score = psum.tile([NQ, w], F32, name=f"score{i}")
            nc.tensor.matmul_mx(
                out=score[:],
                lhsT=q_codes[:].bitcast(FP8X4),
                lhsT_scale=q_scales[:],
                rhs=codes[:].bitcast(FP8X4),
                rhs_scale=scales[:],
                start=True,
                stop=True,
            )
            scores.append(score)

        def reduce(i):
            c0 = starts[i]
            nc.vector.tensor_reduce(
                out=best[:, c0 // SEG:(c0 + WIDTHS[i]) // SEG],
                in_=scores[i][:].rearrange("q (j s) -> q j s", s=SEG),
                axis=AXIS_X,
                op=MAX,
            )

        for i in pieces:
            multiply(i)
            if i >= 2:
                reduce(i - 2)
        for i in pieces[-2:]:
            reduce(i)

        nc.sync.dma_start(out[0], best[:])
